import numpy as np
import ml_dtypes


def mxq(x, axis, fmt="e4m3"):
    dtype, down = {"e4m3": (ml_dtypes.float8_e4m3fn, 7), "e5m2": (ml_dtypes.float8_e5m2, 14)}[fmt]
    v = np.moveaxis(np.asarray(x, np.float32).astype(ml_dtypes.bfloat16).astype(np.float64), axis, -1)
    blocks = v.reshape(v.shape[:-1] + (-1, 32))
    amax = np.abs(blocks).max(-1, keepdims=True)
    byte = np.maximum(np.where(amax > 0, np.frexp(amax)[1] - 1 + 127, 0) - down, 1)
    scale = np.exp2(byte - 127.0)
    codes = (blocks / scale).astype(np.float32).astype(dtype).astype(np.float64)
    return np.moveaxis((codes * scale).reshape(v.shape), -1, axis)


WIDE = False


def mx_kscale(k):
    if not WIDE:
        return np.ones(k)
    levels = np.array([10, -10, 5, -5, 0])
    if k % 512:
        return np.exp2(np.random.permutation(np.resize(levels, k // 32))).repeat(32)
    a = np.empty((k // 512, 16))
    for p in range(k // 512):
        a[p, :8] = np.random.permutation(np.resize(levels, 8))
        for g in range(8):
            far = levels[np.abs(levels - a[p, g]) >= 10]
            a[p, g + 8] = far[np.random.randint(len(far))]
    return np.exp2(a.ravel()).repeat(32)


BF16 = ml_dtypes.bfloat16


def bf(x):
    return np.asarray(x, np.float32).astype(BF16)


def f64(x):
    return np.asarray(x).astype(np.float64)

E4M3FN = np.array([(-1.0 if i & 128 else 1.0) * ((1.0 + (i & 7) / 8.0) * 2.0 ** (((i >> 3) & 15) - 7) if i & 120 else (i & 7) * 2.0 ** -9) for i in range(256)])


def e4m3fn_bytes(y):
    return np.clip(np.asarray(y, np.float64), -448.0, 448.0).astype(np.float32).astype(ml_dtypes.float8_e4m3fn).view(np.uint8)


def e4m3fn_values(b):
    return E4M3FN[b]


S, C = 2048, 512


def setup_inputs():
    t = mx_kscale(S)
    P0 = np.exp(2.0 * np.random.standard_normal((S, S)))
    P0 = P0 / P0.sum(axis=0, keepdims=True)
    P = P0 * t[:, None]
    P_scale = (np.abs(P).max(axis=1, keepdims=True) / 448.0).astype(np.float32)
    P_bytes = e4m3fn_bytes(P / f64(P_scale))
    V = 8.0 * np.random.standard_normal((S, C)) / t[:, None]
    R = 0.25 * np.random.standard_normal((S, C)) / t[:, None]
    discount = np.random.uniform(0.7, 0.99, (S, 1)) / t[:, None]
    return {"P_bytes": P_bytes, "P_scale": P_scale,
            "V": bf(V), "R": bf(R), "discount": bf(discount)}


def reference(P_bytes, P_scale, V, R, discount):
    r, g = f64(R), f64(discount)
    P = e4m3fn_values(P_bytes) * np.repeat(f64(P_scale), S, axis=1)
    p = mxq(P, 0, "e4m3")
    e1 = p.T @ mxq(f64(V), 0, "e4m3")
    v1 = r + g * e1
    e2 = p.T @ mxq(v1, 0, "e4m3")
    return r + g * e2

@@ -1,0 +1,265 @@
+from contextlib import ExitStack
+
+import concourse.mybir as mybir
+from concourse.masks import make_identity
+
+S, C = 2048, 512
+P = 128
+G = 4
+T = 4
+W = 512
+
+F32 = mybir.dt.float32
+BF16 = mybir.dt.bfloat16
+U32 = mybir.dt.uint32
+U8 = mybir.dt.uint8
+FP8 = mybir.dt.float8_e4m3fn
+FP8X4 = mybir.dt.float8_e4m3fn_x4
+MULT = mybir.AluOpType.mult
+ADD = mybir.AluOpType.add
+
+COPY = mybir.ActivationFunctionType.Copy
+SW = [2,2,1,2,4,2,4,1,1,3,1,3,3,3,2,3]
+HL = "SVSVSVSS"
+IL = "PPPPPPPPPPPP"
+
+FLOPS = 2 * 2 * S * S * C
+
+
+def tile_two_sweep_policy_evaluation_d3_kernel(tc, P_bytes, P_scale, V, R, discount, out):
+    nc = tc.nc
+    with ExitStack() as ctx:
+        keep = ctx.enter_context(tc.tile_pool(name="keep", bufs=1))
+        work = ctx.enter_context(tc.tile_pool(name="work", bufs=5))
+        outs = ctx.enter_context(tc.tile_pool(name="outs", bufs=10))
+        psum = ctx.enter_context(tc.psum_pool(name="psum", bufs=8))
+
+        p_scale = keep.tile([P, G * T], F32, name="p_scale")
+        disc = keep.tile([P, G * T], BF16, name="disc")
+        raw01 = [keep.tile([P, G, T, W], U8, name=f"p_bytes_{q}", align_bytes=64) for q in range(2)]
+        raw2 = keep.tile([P, G, T, 2 * W], U8, name="p_bytes_23", align_bytes=64)
+        v_raw = keep.tile([P, G, T, C], BF16, name="v_raw", align_bytes=64)
+        r_sb = keep.tile([P, G, T, C], BF16, name="r_sb", align_bytes=64)
+        p_codes = keep.tile([P, G, G, W], U32, name="p_codes", align_bytes=64)
+        p_planes = keep.tile([P, G, G, W], U8, name="p_planes", align_bytes=64)
+        v_codes = [keep.tile([P, G, C], U32, name=f"v{n}_codes", align_bytes=64) for n in range(2)]
+        v_planes = [keep.tile([P, G, C], U8, name=f"v{n}_planes", align_bytes=64) for n in range(2)]
+
+        ident = keep.tile([P, P], BF16, name="ident")
+        make_identity(nc, ident[:])
+
+        p_view = P_bytes.rearrange("(g p t) i -> g p t i", p=P, t=T)
+        v_view = V.rearrange("(g p t) c -> g p t c", p=P, t=T)
+        r_view = R.rearrange("(g p t) c -> g p t c", p=P, t=T)
+        o_view = out.rearrange("(g p t) c -> g p t c", p=P, t=T)
+
+        def raw(q, g, t):
+            if q < 2:
+                return raw01[q][:, g, t, :]
+            return raw2[:, g, t, (q - 2) * W : (q - 1) * W]
+
+        with tc.manual_schedule():
+            nc.scalar.dma_start(out=p_scale[:], in_=P_scale.rearrange("(g p t) o -> p g (t o)", p=P, t=T))
+            for g in range(G):
+                nc.sync.dma_start(out=raw01[0][:, g], in_=p_view[g][:, :, 0:W])
+                nc.sync.dma_start(out=v_raw[:, g], in_=v_view[g])
+            for g in range(G):
+                nc.sync.dma_start(out=raw01[1][:, g], in_=p_view[g][:, :, W : 2 * W])
+            nc.sync.dma_start(out=disc[:], in_=discount.rearrange("(g p t) o -> p g (t o)", p=P, t=T))
+            nc.sync.dma_start(out=r_sb[:, 0], in_=r_view[0])
+            for g in range(G):
+                nc.sync.dma_start(out=raw2[:, g], in_=p_view[g][:, :, 2 * W : 4 * W])
+            for g in range(1, G):
+                nc.sync.dma_start(out=r_sb[:, g], in_=r_view[g])
+
+            wide = {}
+            ilb = {}
+            inter = {}
+            v_in = {}
+            v1_rows = {}
+            acc1 = {}
+            acc2 = {}
+
+            def widen(n):
+                q, g = divmod(n, G)
+                wide[n] = work.tile([P, T, W], BF16, name=f"wide_{n}", tag="wide", align_bytes=64)
+                for t in range(T):
+                    src = raw(q, g, t).bitcast(FP8)
+                    col = p_scale[:, g * T + t : g * T + t + 1]
+                    if t < SW[n]:
+                        nc.scalar.activation(out=wide[n][:, t, :], in_=src, func=COPY, scale=col)
+                    else:
+                        nc.vector.tensor_scalar(out=wide[n][:, t, :], in0=src, scalar1=col, scalar2=None, op0=MULT)
+
+            def lay_pe(n):
+                if IL[n] != "P":
+                    return
+                src = wide[n][:].rearrange("p t (m b) -> p b m t", b=T)
+                for h in range(2):
+                    ilb[(n, h)] = psum.tile([P, 2 * W], BF16, name=f"ilb_{n}_{h}", tag="bank")
+                    for b in range(2):
+                        nc.tensor.matmul(ilb[(n, h)][:, b * W : (b + 1) * W], lhsT=ident[:], rhs=src[:, 2 * h + b], start=True, stop=True)
+
+            def lay(n):
+                inter[n] = work.tile([P, W * T], BF16, name=f"inter_{n}", tag="inter", align_bytes=64)
+                dst = inter[n][:].rearrange("p (b m t) -> p b m t", b=T, t=T)
+                src = wide[n][:].rearrange("p t (m b) -> p b m t", b=T)
+                if IL[n] == "P":
+                    for h in range(2):
+                        nc.scalar.copy(out=inter[n][:, h * 2 * W : (h + 1) * 2 * W], in_=ilb[(n, h)][:])
+                elif IL[n] == "S":
+                    nc.scalar.copy(out=dst, in_=src)
+                elif IL[n] == "V":
+                    nc.vector.tensor_copy(out=dst, in_=src)
+                else:
+                    nc.scalar.copy(out=dst[:, 2:4], in_=src[:, 2:4])
+                    nc.vector.tensor_copy(out=dst[:, 0:2], in_=src[:, 0:2])
+
+            def quant(n):
+                q, g = divmod(n, G)
+                nc.vector.quantize_mx(out=p_codes[:, q, g, :].bitcast(FP8X4), scales=p_planes[:, q, g, :], in_=inter[n][:])
+
+            def lay_v(sweep, g, eng, c0, c1):
+                key = (sweep, g)
+                if key not in v_in:
+                    v_in[key] = work.tile([P, C, T], BF16, name=f"v{sweep}_in_{g}", tag="v_in", align_bytes=64)
+                src = v_raw[:, g] if sweep == 0 else v1_rows[g][:]
+                eng(out=v_in[key][:, c0:c1, :], in_=src[:, :, c0:c1].rearrange("p t c -> p c t"))
+
+            def lay_half(k):
+                h, g = divmod(k, G)
+                n = 12 + g
+                if n not in inter:
+                    inter[n] = work.tile([P, W * T], BF16, name=f"inter_{n}", tag="inter", align_bytes=64)
+                dst = inter[n][:].rearrange("p (b m t) -> p b m t", b=T, t=T)[:, 2 * h : 2 * h + 2]
+                src = wide[n][:].rearrange("p t (m b) -> p b m t", b=T)[:, 2 * h : 2 * h + 2]
+                if HL[k] == "S":
+                    nc.scalar.copy(out=dst, in_=src)
+                else:
+                    nc.vector.tensor_copy(out=dst, in_=src)
+
+            def quant_half(k):
+                h, g = divmod(k, G)
+                cols = slice(2 * h * P, 2 * (h + 1) * P)
+                nc.vector.quantize_mx(
+                    out=p_codes[:, 3, g, cols].bitcast(FP8X4),
+                    scales=p_planes[:, 3, g, cols],
+                    in_=inter[12 + g][:, 2 * h * T * P : 2 * (h + 1) * T * P],
+                )
+
+            def quant_v(sweep, g):
+                nc.vector.quantize_mx(
+                    out=v_codes[sweep][:, g, :].bitcast(FP8X4),
+                    scales=v_planes[sweep][:, g, :],
+                    in_=v_in[(sweep, g)][:].rearrange("p c t -> p (c t)"),
+                )
+
+            def mm(acc, sweep, q, b, g):
+                cols = slice(b * P, (b + 1) * P)
+                nc.tensor.matmul_mx(
+                    out=acc[:],
+                    lhsT=p_codes[:, q, g, cols].bitcast(FP8X4),
+                    lhsT_scale=p_planes[:, q, g, cols],
+                    rhs=v_codes[sweep][:, g, :].bitcast(FP8X4),
+                    rhs_scale=v_planes[sweep][:, g, :],
+                    start=(g == 0),
+                    stop=(g == G - 1),
+                )
+
+            def bank(name):
+                return psum.tile([P, C], F32, name=name, tag="bank")
+
+            def sweep1(q, b, g):
+                if g == 0:
+                    acc1[(q, b)] = bank(f"acc1_{q}_{b}")
+                mm(acc1[(q, b)], 0, q, b, g)
+
+            def update(dst, acc, q, b):
+                nc.vector.scalar_tensor_tensor(
+                    out=dst, in0=acc[:], scalar=disc[:, q * T + b : q * T + b + 1], in1=r_sb[:, q, b, :], op0=MULT, op1=ADD
+                )
+
+            def evac1(q, b):
+                if b == 0:
+                    v1_rows[q] = work.tile([P, T, C], BF16, name=f"v1_rows_{q}", tag="v1_rows", align_bytes=64)
+                update(v1_rows[q][:, b, :], acc1[(q, b)], q, b)
+
+            def sweep2(i, gs):
+                q, b = divmod(i, T)
+                for g in gs:
+                    if g == 0:
+                        acc2[i] = bank(f"acc2_{i}")
+                    mm(acc2[i], 1, q, b, g)
+
+            def evac2(i):
+                q, b = divmod(i, T)
+                o = outs.tile([P, C], F32, name=f"out_{i}", tag="o")
+                update(o[:], acc2[i], q, b)
+                nc.sync.dma_start(out=o_view[q][:, b, :], in_=o[:])
+
+            widen(0)
+            lay_pe(0)
+            lay_v(0, 0, nc.vector.tensor_copy, 0, C)
+            widen(1)
+            lay_pe(1)
+            lay(0)
+            quant_v(0, 0)
+            lay_v(0, 1, nc.vector.tensor_copy, 0, C)
+            widen(2)
+            for n in range(12):
+                q, g = divmod(n, G)
+                if q >= 1 and g == 0:
+                    for b in range(T):
+                        evac1(q - 1, b)
+                if n + 2 < 12:
+                    lay_pe(n + 2)
+                if n + 1 < 12:
+                    lay(n + 1)
+                quant(n)
+                widen(n + 3)
+                if n < G:
+                    if n:
+                        quant_v(0, n)
+                    if 1 <= n + 1 < G and n:
+                        lay_v(0, n + 1, nc.vector.tensor_copy, 0, C)
+                if q >= 1 and g == 1:
+                    lay_v(1, q - 1, nc.vector.tensor_copy, 0, C)
+                if q >= 1 and g == 2:
+                    quant_v(1, q - 1)
+                for b in range(T):
+                    sweep1(q, b, g)
+            lay_half(0)
+            for b in range(T):
+                evac1(2, b)
+            widen(15)
+            for k in range(8):
+                h, g = divmod(k, G)
+                if k < 7:
+                    lay_half(k + 1)
+                quant_half(k)
+                if k == 0:
+                    lay_v(1, 2, nc.vector.tensor_copy, 0, C)
+                if k == 2:
+                    quant_v(1, 2)
+                if k == 5:
+                    evac1(3, 0)
+                    evac1(3, 1)
+                for b in (2 * h, 2 * h + 1):
+                    sweep1(3, b, g)
+                if k < 4:
+                    sweep2(k, [0, 1])
+                if 4 <= k:
+                    sweep2(k - 4, [2])
+            for b in (2, 3):
+                evac1(3, b)
+            for i in range(4, 8):
+                sweep2(i, [0, 1, 2])
+            lay_v(1, 3, nc.scalar.copy, 320, C)
+            lay_v(1, 3, nc.vector.tensor_copy, 0, 320)
+            quant_v(1, 3)
+            for i in range(8):
+                sweep2(i, [3])
+                evac2(i)
+            for i in range(8, 16):
+                sweep2(i, range(G))
+                evac2(i)

@@ -19,9 +19,16 @@ MULT = mybir.AluOpType.mult
 ADD = mybir.AluOpType.add
 
 COPY = mybir.ActivationFunctionType.Copy
-SW = [2,2,1,2,4,2,4,1,1,3,1,3,3,3,2,3]
-HL = "SVSVSVSS"
-IL = "PPPPPPPPPPPP"
+SW = [0,3,0,2,1,2,0,0,0,0,0,0,3,1,3,2]
+BT = [0, 1, 2, 3, 4]
+PB = {11: [0]}
+PBK = {0: [1], 1: [2], 2: [3], 3: [4]}
+PA = {0: [(5, [0, 1])], 1: [(6, [0, 1])], 2: [(7, [0, 1])], 3: [(8, [0, 1])], 4: [(5, [2]), (6, [2])], 5: [(7, [2]), (8, [2])], 6: [(9, [0, 1, 2])], 7: []}
+PT = [(10, [0, 1, 2]), (11, [0, 1, 2]), (12, [0, 1, 2])]
+DONE = {i: [0, 1, 2] if i <= 12 else [] for i in range(16)}
+ORDER = [0, 5, 13, 1, 6, 2, 7, 14, 3, 8, 4, 9, 15, 10, 11, 12]
+HL = "SSSVSSVS"
+IL = "SMMSSSSSSSSS"
 
 FLOPS = 2 * 2 * S * S * C
 
@@ -35,7 +42,8 @@ def tile_two_sweep_policy_evaluation_d3_kernel(tc, P_bytes, P_scale, V, R, disco
         psum = ctx.enter_context(tc.psum_pool(name="psum", bufs=8))
 
         p_scale = keep.tile([P, G * T], F32, name="p_scale")
-        disc = keep.tile([P, G * T], BF16, name="disc")
+        disc_in = keep.tile([P, G * T], BF16, name="disc_in")
+        disc = keep.tile([P, G * T], F32, name="disc")
         raw01 = [keep.tile([P, G, T, W], U8, name=f"p_bytes_{q}", align_bytes=64) for q in range(2)]
         raw2 = keep.tile([P, G, T, 2 * W], U8, name="p_bytes_23", align_bytes=64)
         v_raw = keep.tile([P, G, T, C], BF16, name="v_raw", align_bytes=64)
@@ -65,7 +73,7 @@ def tile_two_sweep_policy_evaluation_d3_kernel(tc, P_bytes, P_scale, V, R, disco
                 nc.sync.dma_start(out=v_raw[:, g], in_=v_view[g])
             for g in range(G):
                 nc.sync.dma_start(out=raw01[1][:, g], in_=p_view[g][:, :, W : 2 * W])
-            nc.sync.dma_start(out=disc[:], in_=discount.rearrange("(g p t) o -> p g (t o)", p=P, t=T))
+            nc.sync.dma_start(out=disc_in[:], in_=discount.rearrange("(g p t) o -> p g (t o)", p=P, t=T))
             nc.sync.dma_start(out=r_sb[:, 0], in_=r_view[0])
             for g in range(G):
                 nc.sync.dma_start(out=raw2[:, g], in_=p_view[g][:, :, 2 * W : 4 * W])
@@ -73,6 +81,7 @@ def tile_two_sweep_policy_evaluation_d3_kernel(tc, P_bytes, P_scale, V, R, disco
                 nc.sync.dma_start(out=r_sb[:, g], in_=r_view[g])
 
             wide = {}
+            part = {}
             ilb = {}
             inter = {}
             v_in = {}
@@ -100,10 +109,15 @@ def tile_two_sweep_policy_evaluation_d3_kernel(tc, P_bytes, P_scale, V, R, disco
                     for b in range(2):
                         nc.tensor.matmul(ilb[(n, h)][:, b * W : (b + 1) * W], lhsT=ident[:], rhs=src[:, 2 * h + b], start=True, stop=True)
 
+            def il_views(n):
+                return (
+                    inter[n][:].rearrange("p (b m e t) -> p m b e t", b=T, e=2, t=T),
+                    wide[n][:].rearrange("p t (m e b) -> p m b e t", e=2, b=T),
+                )
+
             def lay(n):
                 inter[n] = work.tile([P, W * T], BF16, name=f"inter_{n}", tag="inter", align_bytes=64)
-                dst = inter[n][:].rearrange("p (b m t) -> p b m t", b=T, t=T)
-                src = wide[n][:].rearrange("p t (m b) -> p b m t", b=T)
+                dst, src = il_views(n)
                 if IL[n] == "P":
                     for h in range(2):
                         nc.scalar.copy(out=inter[n][:, h * 2 * W : (h + 1) * 2 * W], in_=ilb[(n, h)][:])
@@ -112,8 +126,8 @@ def tile_two_sweep_policy_evaluation_d3_kernel(tc, P_bytes, P_scale, V, R, disco
                 elif IL[n] == "V":
                     nc.vector.tensor_copy(out=dst, in_=src)
                 else:
-                    nc.scalar.copy(out=dst[:, 2:4], in_=src[:, 2:4])
-                    nc.vector.tensor_copy(out=dst[:, 0:2], in_=src[:, 0:2])
+                    nc.scalar.copy(out=dst[:, 40:], in_=src[:, 40:])
+                    nc.vector.tensor_copy(out=dst[:, :40], in_=src[:, :40])
 
             def quant(n):
                 q, g = divmod(n, G)
@@ -122,7 +136,7 @@ def tile_two_sweep_policy_evaluation_d3_kernel(tc, P_bytes, P_scale, V, R, disco
             def lay_v(sweep, g, eng, c0, c1):
                 key = (sweep, g)
                 if key not in v_in:
-                    v_in[key] = work.tile([P, C, T], BF16, name=f"v{sweep}_in_{g}", tag="v_in", align_bytes=64)
+                    v_in[key] = work.tile([P, C, T], BF16, name=f"v{sweep}_in_{g}", tag="v_in", align_bytes=64, bufs=2)
                 src = v_raw[:, g] if sweep == 0 else v1_rows[g][:]
                 eng(out=v_in[key][:, c0:c1, :], in_=src[:, :, c0:c1].rearrange("p t c -> p c t"))
 
@@ -131,8 +145,8 @@ def tile_two_sweep_policy_evaluation_d3_kernel(tc, P_bytes, P_scale, V, R, disco
                 n = 12 + g
                 if n not in inter:
                     inter[n] = work.tile([P, W * T], BF16, name=f"inter_{n}", tag="inter", align_bytes=64)
-                dst = inter[n][:].rearrange("p (b m t) -> p b m t", b=T, t=T)[:, 2 * h : 2 * h + 2]
-                src = wide[n][:].rearrange("p t (m b) -> p b m t", b=T)[:, 2 * h : 2 * h + 2]
+                dst, src = il_views(n)
+                dst, src = dst[:, :, 2 * h : 2 * h + 2], src[:, :, 2 * h : 2 * h + 2]
                 if HL[k] == "S":
                     nc.scalar.copy(out=dst, in_=src)
                 else:
@@ -154,7 +168,7 @@ def tile_two_sweep_policy_evaluation_d3_kernel(tc, P_bytes, P_scale, V, R, disco
                     in_=v_in[(sweep, g)][:].rearrange("p c t -> p (c t)"),
                 )
 
-            def mm(acc, sweep, q, b, g):
+            def mm(acc, sweep, q, b, g, first=0, last=G - 1):
                 cols = slice(b * P, (b + 1) * P)
                 nc.tensor.matmul_mx(
                     out=acc[:],
@@ -162,12 +176,20 @@ def tile_two_sweep_policy_evaluation_d3_kernel(tc, P_bytes, P_scale, V, R, disco
                     lhsT_scale=p_planes[:, q, g, cols],
                     rhs=v_codes[sweep][:, g, :].bitcast(FP8X4),
                     rhs_scale=v_planes[sweep][:, g, :],
-                    start=(g == 0),
-                    stop=(g == G - 1),
+                    start=(g == first),
+                    stop=(g == last),
                 )
 
+            free = list(range(8))
+            held = {}
+
             def bank(name):
-                return psum.tile([P, C], F32, name=name, tag="bank")
+                b = free.pop(0)
+                held[name] = b
+                return psum.tile([P, C], F32, name=name, tag=f"bank_{b}", bufs=1)
+
+            def give(name):
+                free.append(held[name])
 
             def sweep1(q, b, g):
                 if g == 0:
@@ -181,20 +203,37 @@ def tile_two_sweep_policy_evaluation_d3_kernel(tc, P_bytes, P_scale, V, R, disco
 
             def evac1(q, b):
                 if b == 0:
-                    v1_rows[q] = work.tile([P, T, C], BF16, name=f"v1_rows_{q}", tag="v1_rows", align_bytes=64)
+                    v1_rows[q] = work.tile([P, T, C], BF16, name=f"v1_rows_{q}", tag="v1_rows", align_bytes=64, bufs=2)
                 update(v1_rows[q][:, b, :], acc1[(q, b)], q, b)
+                give(f"acc1_{q}_{b}")
 
-            def sweep2(i, gs):
+            def sweep2(i, gs, first=0, last=G - 1):
                 q, b = divmod(i, T)
                 for g in gs:
-                    if g == 0:
-                        acc2[i] = bank(f"acc2_{i}")
-                    mm(acc2[i], 1, q, b, g)
+                    if g == first:
+                        acc2[i] = bank(f"acc2_{i}_{g}")
+                    mm(acc2[i], 1, q, b, g, first, last)
+
+            def spill(i):
+                q, b = divmod(i, T)
+                part[i] = keep.tile([P, C], F32, name=f"part_{i}")
+                nc.scalar.activation(out=part[i][:], in_=acc2[i][:], func=COPY, scale=disc[:, i : i + 1])
+                give(f"acc2_{i}_0")
+
+            def evac2b(i):
+                q, b = divmod(i, T)
+                o1 = outs.tile([P, C], F32, name=f"sum_{i}", tag="sum", bufs=3)
+                nc.vector.scalar_tensor_tensor(out=o1[:], in0=acc2[i][:], scalar=disc[:, i : i + 1], in1=part[i][:], op0=MULT, op1=ADD)
+                give(f"acc2_{i}_2")
+                o = outs.tile([P, C], F32, name=f"out_{i}", tag="o")
+                nc.gpsimd.tensor_tensor(out=o[:], in0=o1[:], in1=r_sb[:, q, b, :], op=ADD)
+                nc.sync.dma_start(out=o_view[q][:, b, :], in_=o[:])
 
             def evac2(i):
                 q, b = divmod(i, T)
                 o = outs.tile([P, C], F32, name=f"out_{i}", tag="o")
                 update(o[:], acc2[i], q, b)
+                give(f"acc2_{i}_0")
                 nc.sync.dma_start(out=o_view[q][:, b, :], in_=o[:])
 
             widen(0)
@@ -208,6 +247,8 @@ def tile_two_sweep_policy_evaluation_d3_kernel(tc, P_bytes, P_scale, V, R, disco
             widen(2)
             for n in range(12):
                 q, g = divmod(n, G)
+                if n == 3:
+                    nc.vector.tensor_copy(out=disc[:], in_=disc_in[:])
                 if q >= 1 and g == 0:
                     for b in range(T):
                         evac1(q - 1, b)

@@ -19,16 +19,11 @@ MULT = mybir.AluOpType.mult
 ADD = mybir.AluOpType.add
 
 COPY = mybir.ActivationFunctionType.Copy
-SW = [0,3,0,2,1,2,0,0,0,0,0,0,3,1,3,2]
-BT = [0, 1, 2, 3, 4]
-PB = {11: [0]}
-PBK = {0: [1], 1: [2], 2: [3], 3: [4]}
-PA = {0: [(5, [0, 1])], 1: [(6, [0, 1])], 2: [(7, [0, 1])], 3: [(8, [0, 1])], 4: [(5, [2]), (6, [2])], 5: [(7, [2]), (8, [2])], 6: [(9, [0, 1, 2])], 7: []}
-PT = [(10, [0, 1, 2]), (11, [0, 1, 2]), (12, [0, 1, 2])]
-DONE = {i: [0, 1, 2] if i <= 12 else [] for i in range(16)}
-ORDER = [0, 5, 13, 1, 6, 2, 7, 14, 3, 8, 4, 9, 15, 10, 11, 12]
-HL = "SSSVSSVS"
-IL = "SMMSSSSSSSSS"
+SW = [2,4,4,3,3,4,3,4,4,4,3,4,4,4,4,4]
+VIL = "VVSV"
+V1IL = "SSS"
+HL = "VVVSVVSS"
+IL = "VVVVVVVVVVVV"
 
 FLOPS = 2 * 2 * S * S * C
 
@@ -80,6 +75,7 @@ def tile_two_sweep_policy_evaluation_d3_kernel(tc, P_bytes, P_scale, V, R, disco
             for g in range(1, G):
                 nc.sync.dma_start(out=r_sb[:, g], in_=r_view[g])
 
+            COPIER = {"V": nc.vector.tensor_copy, "S": nc.scalar.copy}
             wide = {}
             part = {}
             ilb = {}
@@ -238,12 +234,12 @@ def tile_two_sweep_policy_evaluation_d3_kernel(tc, P_bytes, P_scale, V, R, disco
 
             widen(0)
             lay_pe(0)
-            lay_v(0, 0, nc.vector.tensor_copy, 0, C)
+            lay_v(0, 0, COPIER[VIL[0]], 0, C)
             widen(1)
             lay_pe(1)
             lay(0)
             quant_v(0, 0)
-            lay_v(0, 1, nc.vector.tensor_copy, 0, C)
+            lay_v(0, 1, COPIER[VIL[1]], 0, C)
             widen(2)
             for n in range(12):
                 q, g = divmod(n, G)
@@ -262,9 +258,9 @@ def tile_two_sweep_policy_evaluation_d3_kernel(tc, P_bytes, P_scale, V, R, disco
                     if n:
                         quant_v(0, n)
                     if 1 <= n + 1 < G and n:
-                        lay_v(0, n + 1, nc.vector.tensor_copy, 0, C)
+                        lay_v(0, n + 1, COPIER[VIL[n + 1]], 0, C)
                 if q >= 1 and g == 1:
-                    lay_v(1, q - 1, nc.vector.tensor_copy, 0, C)
+                    lay_v(1, q - 1, COPIER[V1IL[q - 1]], 0, C)
                 if q >= 1 and g == 2:
                     quant_v(1, q - 1)
                 for b in range(T):
@@ -279,7 +275,7 @@ def tile_two_sweep_policy_evaluation_d3_kernel(tc, P_bytes, P_scale, V, R, disco
                     lay_half(k + 1)
                 quant_half(k)
                 if k == 0:
-                    lay_v(1, 2, nc.vector.tensor_copy, 0, C)
+                    lay_v(1, 2, COPIER[V1IL[2]], 0, C)
                 if k == 2:
                     quant_v(1, 2)
                 if k == 5:

@@ -19,10 +19,10 @@ MULT = mybir.AluOpType.mult
 ADD = mybir.AluOpType.add
 
 COPY = mybir.ActivationFunctionType.Copy
-SW = [2,4,4,3,3,4,3,4,4,4,3,4,4,4,4,4]
+SW = [1,4,4,3,3,4,4,4,4,4,3,3,4,4,4,4]
 VIL = "VVSV"
-V1IL = "SSS"
-HL = "VVVSVVSS"
+V1IL = "SSV"
+HL = "VVVSSSVS"
 IL = "VVVVVVVVVVVV"
 
 FLOPS = 2 * 2 * S * S * C
@@ -36,7 +36,8 @@ def tile_two_sweep_policy_evaluation_d3_kernel(tc, P_bytes, P_scale, V, R, disco
         outs = ctx.enter_context(tc.tile_pool(name="outs", bufs=10))
         psum = ctx.enter_context(tc.psum_pool(name="psum", bufs=8))
 
-        p_scale = keep.tile([P, G * T], F32, name="p_scale")
+        first_scale = keep.tile([P, T], F32, name="first_scale")
+        rest_scale = keep.tile([P, G - 1, T], F32, name="rest_scale")
         disc_in = keep.tile([P, G * T], BF16, name="disc_in")
         disc = keep.tile([P, G * T], F32, name="disc")
         raw01 = [keep.tile([P, G, T, W], U8, name=f"p_bytes_{q}", align_bytes=64) for q in range(2)]
@@ -62,9 +63,15 @@ def tile_two_sweep_policy_evaluation_d3_kernel(tc, P_bytes, P_scale, V, R, disco
             return raw2[:, g, t, (q - 2) * W : (q - 1) * W]
 
         with tc.manual_schedule():
-            nc.scalar.dma_start(out=p_scale[:], in_=P_scale.rearrange("(g p t) o -> p g (t o)", p=P, t=T))
+            s_view = P_scale.rearrange("(g p t) o -> g p (t o)", p=P, t=T)
+            nc.scalar.dma_start(out=first_scale[:], in_=s_view[0])
             for g in range(G):
                 nc.sync.dma_start(out=raw01[0][:, g], in_=p_view[g][:, :, 0:W])
+                if g == 0:
+                    nc.sync.dma_start(
+                        out=rest_scale[:],
+                        in_=P_scale.rearrange("(g p t) o -> p g (t o)", p=P, t=T)[:, 1:],
+                    )
                 nc.sync.dma_start(out=v_raw[:, g], in_=v_view[g])
             for g in range(G):
                 nc.sync.dma_start(out=raw01[1][:, g], in_=p_view[g][:, :, W : 2 * W])
@@ -76,8 +83,12 @@ def tile_two_sweep_policy_evaluation_d3_kernel(tc, P_bytes, P_scale, V, R, disco
                 nc.sync.dma_start(out=r_sb[:, g], in_=r_view[g])
 
             COPIER = {"V": nc.vector.tensor_copy, "S": nc.scalar.copy}
+            free = list(range(8))
+            held = {}
             wide = {}
             part = {}
+            done_half = {}
+            HC = C // 2
             ilb = {}
             inter = {}
             v_in = {}
@@ -90,7 +101,7 @@ def tile_two_sweep_policy_evaluation_d3_kernel(tc, P_bytes, P_scale, V, R, disco
                 wide[n] = work.tile([P, T, W], BF16, name=f"wide_{n}", tag="wide", align_bytes=64)
                 for t in range(T):
                     src = raw(q, g, t).bitcast(FP8)
-                    col = p_scale[:, g * T + t : g * T + t + 1]
+                    col = first_scale[:, t : t + 1] if g == 0 else rest_scale[:, g - 1, t : t + 1]
                     if t < SW[n]:
                         nc.scalar.activation(out=wide[n][:, t, :], in_=src, func=COPY, scale=col)
                     else:
@@ -99,11 +110,19 @@ def tile_two_sweep_policy_evaluation_d3_kernel(tc, P_bytes, P_scale, V, R, disco
             def lay_pe(n):
                 if IL[n] != "P":
                     return
-                src = wide[n][:].rearrange("p t (m b) -> p b m t", b=T)
                 for h in range(2):
-                    ilb[(n, h)] = psum.tile([P, 2 * W], BF16, name=f"ilb_{n}_{h}", tag="bank")
-                    for b in range(2):
-                        nc.tensor.matmul(ilb[(n, h)][:, b * W : (b + 1) * W], lhsT=ident[:], rhs=src[:, 2 * h + b], start=True, stop=True)
+                    b = free.pop(0)
+                    ilb[(n, h)] = psum.tile([P, 2 * W], BF16, name=f"ilb_{n}_{h}", tag=f"bank_{b}", bufs=1)
+                    held[("il", n, h)] = b
+                    for k in range(2):
+                        i0 = (2 * h + k) * P
+                        nc.tensor.matmul(
+                            ilb[(n, h)][:, k * W : (k + 1) * W].rearrange("p (b m t) -> p m t b", b=T, t=T),
+                            lhsT=ident[:],
+                            rhs=wide[n][:, :, i0 : i0 + P].rearrange("p t (m b) -> p m t b", b=T),
+                            start=True,
+                            stop=True,
+                        )
 
             def il_views(n):
                 return (
@@ -116,7 +135,11 @@ def tile_two_sweep_policy_evaluation_d3_kernel(tc, P_bytes, P_scale, V, R, disco
                 dst, src = il_views(n)
                 if IL[n] == "P":
                     for h in range(2):
-                        nc.scalar.copy(out=inter[n][:, h * 2 * W : (h + 1) * 2 * W], in_=ilb[(n, h)][:])
+                        nc.scalar.copy(
+                            out=inter[n][:].rearrange("p (b h k x) -> p h k b x", b=T, h=2, k=2)[:, h],
+                            in_=ilb[(n, h)][:].rearrange("p (k b x) -> p k b x", k=2, b=T),
+                        )
+                        give(("il", n, h))
                 elif IL[n] == "S":
                     nc.scalar.copy(out=dst, in_=src)
                 elif IL[n] == "V":
@@ -176,9 +199,6 @@ def tile_two_sweep_policy_evaluation_d3_kernel(tc, P_bytes, P_scale, V, R, disco
                     stop=(g == last),
                 )
 
-            free = list(range(8))
-            held = {}
-
             def bank(name):
                 b = free.pop(0)
                 held[name] = b
@@ -209,6 +229,27 @@ def tile_two_sweep_policy_evaluation_d3_kernel(tc, P_bytes, P_scale, V, R, disco
                     if g == first:
                         acc2[i] = bank(f"acc2_{i}_{g}")
                     mm(acc2[i], 1, q, b, g, first, last)
+
+            def evac1_half(q, b, half):
+                c = slice(half * HC, (half + 1) * HC)
+                if b not in done_half.setdefault(q, []):
+                    done_half[q].append(b)
+                nc.vector.scalar_tensor_tensor(
+                    out=v1_get(q)[:, b, c], in0=acc1[(q, b)][:, c], scalar=disc[:, q * T + b : q * T + b + 1], in1=r_sb[:, q, b, c], op0=MULT, op1=ADD
+                )
+                if half == 1:
+                    give(f"acc1_{q}_{b}")
+
+            def v1_get(q):
+                return v1_rows[q]
+
+            def quant_v_half(sweep, g, half):
+                c = slice(half * HC, (half + 1) * HC)
+                nc.vector.quantize_mx(
+                    out=v_codes[sweep][:, g, c].bitcast(FP8X4),
+                    scales=v_planes[sweep][:, g, c],
+                    in_=v_in[(sweep, g)][:, c, :].rearrange("p c t -> p (c t)"),
+                )
 
             def spill(i):
                 q, b = divmod(i, T)
@@ -245,14 +286,14 @@ def tile_two_sweep_policy_evaluation_d3_kernel(tc, P_bytes, P_scale, V, R, disco
                 q, g = divmod(n, G)
                 if n == 3:
                     nc.vector.tensor_copy(out=disc[:], in_=disc_in[:])
-                if q >= 1 and g == 0:
-                    for b in range(T):
-                        evac1(q - 1, b)
                 if n + 2 < 12:
                     lay_pe(n + 2)
                 if n + 1 < 12:
                     lay(n + 1)
                 quant(n)
+                if q >= 1 and g == 0:
+                    for b in range(T):
+                        evac1(q - 1, b)
                 widen(n + 3)
                 if n < G:
                     if n:
@@ -266,8 +307,6 @@ def tile_two_sweep_policy_evaluation_d3_kernel(tc, P_bytes, P_scale, V, R, disco
                 for b in range(T):
                     sweep1(q, b, g)
             lay_half(0)
-            for b in range(T):
-                evac1(2, b)
             widen(15)
             for k in range(8):
                 h, g = divmod(k, G)
@@ -275,6 +314,9 @@ def tile_two_sweep_policy_evaluation_d3_kernel(tc, P_bytes, P_scale, V, R, disco
                     lay_half(k + 1)
                 quant_half(k)
                 if k == 0:
+                    for b in range(T):
+                        evac1(2, b)
+                if k == 1:
                     lay_v(1, 2, COPIER[V1IL[2]], 0, C)
                 if k == 2:
                     quant_v(1, 2)
@@ -285,15 +327,19 @@ def tile_two_sweep_policy_evaluation_d3_kernel(tc, P_bytes, P_scale, V, R, disco
                     sweep1(3, b, g)
                 if k < 4:
                     sweep2(k, [0, 1])
-                if 4 <= k:
+                if k in (4, 5):
                     sweep2(k - 4, [2])
-            for b in (2, 3):
-                evac1(3, b)
+            for half in range(2):
+                for b in (2, 3):
+                    evac1_half(3, b, half)
+            for i in (2, 3):
+                sweep2(i, [2])
             for i in range(4, 8):
                 sweep2(i, [0, 1, 2])
-            lay_v(1, 3, nc.scalar.copy, 320, C)
-            lay_v(1, 3, nc.vector.tensor_copy, 0, 320)
-            quant_v(1, 3)
+            lay_v(1, 3, nc.scalar.copy, 0, HC)
+            lay_v(1, 3, nc.vector.tensor_copy, HC, C)
+            for half in range(2):
+                quant_v_half(1, 3, half)
             for i in range(8):
                 sweep2(i, [3])
                 evac2(i)

@@ -1,13 +1,13 @@
 from contextlib import ExitStack
 
 import concourse.mybir as mybir
-from concourse.masks import make_identity
 
 S, C = 2048, 512
 P = 128
-G = 4
 T = 4
-W = 512
+W = P * T
+G = S // W
+HALF = C // 2
 
 F32 = mybir.dt.float32
 BF16 = mybir.dt.bfloat16
@@ -17,332 +17,213 @@ FP8 = mybir.dt.float8_e4m3fn
 FP8X4 = mybir.dt.float8_e4m3fn_x4
 MULT = mybir.AluOpType.mult
 ADD = mybir.AluOpType.add
-
 COPY = mybir.ActivationFunctionType.Copy
-SW = [1,4,4,3,3,4,4,4,4,4,3,3,4,4,4,4]
-VIL = "VVSV"
-V1IL = "SSV"
-HL = "VVVSSSVS"
-IL = "VVVVVVVVVVVV"
 
 FLOPS = 2 * 2 * S * S * C
+
+SCALAR_SLOTS = [1] + [4, 4, 3] + [4, 4, 4, 3] + [4, 4, 4, 3] + [4, 4, 4, 4]
+V_BY = "VVSV"
+V1_BY = "SSV"
+LAST_BY = "VVVSSSVS"
 
 
 def tile_two_sweep_policy_evaluation_d3_kernel(tc, P_bytes, P_scale, V, R, discount, out):
     nc = tc.nc
+    copier = {"V": nc.vector.tensor_copy, "S": nc.scalar.copy}
+
     with ExitStack() as ctx:
         keep = ctx.enter_context(tc.tile_pool(name="keep", bufs=1))
-        work = ctx.enter_context(tc.tile_pool(name="work", bufs=5))
-        outs = ctx.enter_context(tc.tile_pool(name="outs", bufs=10))
+        chunks = ctx.enter_context(tc.tile_pool(name="chunks", bufs=5))
+        rows = ctx.enter_context(tc.tile_pool(name="rows", bufs=2))
+        results = ctx.enter_context(tc.tile_pool(name="results", bufs=10))
         psum = ctx.enter_context(tc.psum_pool(name="psum", bufs=8))
 
-        first_scale = keep.tile([P, T], F32, name="first_scale")
-        rest_scale = keep.tile([P, G - 1, T], F32, name="rest_scale")
-        disc_in = keep.tile([P, G * T], BF16, name="disc_in")
-        disc = keep.tile([P, G * T], F32, name="disc")
-        raw01 = [keep.tile([P, G, T, W], U8, name=f"p_bytes_{q}", align_bytes=64) for q in range(2)]
-        raw2 = keep.tile([P, G, T, 2 * W], U8, name="p_bytes_23", align_bytes=64)
+        scale_0 = keep.tile([P, T], F32, name="scale_0")
+        scale_rest = keep.tile([P, G - 1, T], F32, name="scale_rest")
+        disc = keep.tile([P, G, T], BF16, name="disc")
+        bytes_q = [keep.tile([P, G, T, W], U8, name=f"bytes_{q}", align_bytes=64) for q in range(2)]
+        bytes_23 = keep.tile([P, G, T, 2 * W], U8, name="bytes_23", align_bytes=64)
         v_raw = keep.tile([P, G, T, C], BF16, name="v_raw", align_bytes=64)
         r_sb = keep.tile([P, G, T, C], BF16, name="r_sb", align_bytes=64)
         p_codes = keep.tile([P, G, G, W], U32, name="p_codes", align_bytes=64)
-        p_planes = keep.tile([P, G, G, W], U8, name="p_planes", align_bytes=64)
-        v_codes = [keep.tile([P, G, C], U32, name=f"v{n}_codes", align_bytes=64) for n in range(2)]
-        v_planes = [keep.tile([P, G, C], U8, name=f"v{n}_planes", align_bytes=64) for n in range(2)]
+        p_scales = keep.tile([P, G, G, W], U8, name="p_scales", align_bytes=64)
+        v_codes = [keep.tile([P, G, C], U32, name=f"v_codes_{s}", align_bytes=64) for s in range(2)]
+        v_scales = [keep.tile([P, G, C], U8, name=f"v_scales_{s}", align_bytes=64) for s in range(2)]
 
-        ident = keep.tile([P, P], BF16, name="ident")
-        make_identity(nc, ident[:])
-
+        scale_view = P_scale.rearrange("(g p t) o -> p g (t o)", p=P, t=T)
         p_view = P_bytes.rearrange("(g p t) i -> g p t i", p=P, t=T)
         v_view = V.rearrange("(g p t) c -> g p t c", p=P, t=T)
         r_view = R.rearrange("(g p t) c -> g p t c", p=P, t=T)
-        o_view = out.rearrange("(g p t) c -> g p t c", p=P, t=T)
+        out_view = out.rearrange("(g p t) c -> g p t c", p=P, t=T)
 
-        def raw(q, g, t):
-            if q < 2:
-                return raw01[q][:, g, t, :]
-            return raw2[:, g, t, (q - 2) * W : (q - 1) * W]
+        nc.scalar.dma_start(out=scale_0[:], in_=scale_view[:, 0])
+        nc.sync.dma_start(out=bytes_q[0][:, 0], in_=p_view[0][:, :, 0:W])
+        nc.sync.dma_start(out=scale_rest[:], in_=scale_view[:, 1:])
+        nc.sync.dma_start(out=v_raw[:, 0], in_=v_view[0])
+        for g in range(1, G):
+            nc.sync.dma_start(out=bytes_q[0][:, g], in_=p_view[g][:, :, 0:W])
+            nc.sync.dma_start(out=v_raw[:, g], in_=v_view[g])
+        for g in range(G):
+            nc.sync.dma_start(out=bytes_q[1][:, g], in_=p_view[g][:, :, W : 2 * W])
+        nc.sync.dma_start(out=disc[:], in_=discount.rearrange("(g p t) o -> p g (t o)", p=P, t=T))
+        nc.sync.dma_start(out=r_sb[:, 0], in_=r_view[0])
+        for g in range(G):
+            nc.sync.dma_start(out=bytes_23[:, g], in_=p_view[g][:, :, 2 * W :])
+        for q in range(1, G):
+            nc.sync.dma_start(out=r_sb[:, q], in_=r_view[q])
 
-        with tc.manual_schedule():
-            s_view = P_scale.rearrange("(g p t) o -> g p (t o)", p=P, t=T)
-            nc.scalar.dma_start(out=first_scale[:], in_=s_view[0])
-            for g in range(G):
-                nc.sync.dma_start(out=raw01[0][:, g], in_=p_view[g][:, :, 0:W])
-                if g == 0:
-                    nc.sync.dma_start(
-                        out=rest_scale[:],
-                        in_=P_scale.rearrange("(g p t) o -> p g (t o)", p=P, t=T)[:, 1:],
+        wide = {}
+        mixed = {}
+        v_mixed = {}
+        v1_rows = {}
+        acc = {}
+
+        def widen(n):
+            q, g = divmod(n, G)
+            wide[n] = chunks.tile([P, T, W], BF16, name=f"wide_{n}", tag="wide", align_bytes=64)
+            for t in range(T):
+                src = bytes_q[q][:, g, t, :] if q < 2 else bytes_23[:, g, t, (q - 2) * W : (q - 1) * W]
+                scale = scale_0[:, t : t + 1] if g == 0 else scale_rest[:, g - 1, t : t + 1]
+                if t < SCALAR_SLOTS[n]:
+                    nc.scalar.activation(out=wide[n][:, t, :], in_=src.bitcast(FP8), func=COPY, scale=scale)
+                else:
+                    nc.vector.tensor_scalar(
+                        out=wide[n][:, t, :], in0=src.bitcast(FP8), scalar1=scale, scalar2=None, op0=MULT
                     )
-                nc.sync.dma_start(out=v_raw[:, g], in_=v_view[g])
-            for g in range(G):
-                nc.sync.dma_start(out=raw01[1][:, g], in_=p_view[g][:, :, W : 2 * W])
-            nc.sync.dma_start(out=disc_in[:], in_=discount.rearrange("(g p t) o -> p g (t o)", p=P, t=T))
-            nc.sync.dma_start(out=r_sb[:, 0], in_=r_view[0])
-            for g in range(G):
-                nc.sync.dma_start(out=raw2[:, g], in_=p_view[g][:, :, 2 * W : 4 * W])
-            for g in range(1, G):
-                nc.sync.dma_start(out=r_sb[:, g], in_=r_view[g])
 
-            COPIER = {"V": nc.vector.tensor_copy, "S": nc.scalar.copy}
-            free = list(range(8))
-            held = {}
-            wide = {}
-            part = {}
-            done_half = {}
-            HC = C // 2
-            ilb = {}
-            inter = {}
-            v_in = {}
-            v1_rows = {}
-            acc1 = {}
-            acc2 = {}
+        def interleave(n, b0, b1, copy):
+            if n not in mixed:
+                mixed[n] = chunks.tile([P, W * T], BF16, name=f"mixed_{n}", tag="mixed", align_bytes=64)
+            copy(
+                out=mixed[n][:].rearrange("p (b m e t) -> p m b e t", b=T, e=2, t=T)[:, :, b0:b1],
+                in_=wide[n][:].rearrange("p t (m e b) -> p m b e t", e=2, b=T)[:, :, b0:b1],
+            )
 
-            def widen(n):
-                q, g = divmod(n, G)
-                wide[n] = work.tile([P, T, W], BF16, name=f"wide_{n}", tag="wide", align_bytes=64)
-                for t in range(T):
-                    src = raw(q, g, t).bitcast(FP8)
-                    col = first_scale[:, t : t + 1] if g == 0 else rest_scale[:, g - 1, t : t + 1]
-                    if t < SW[n]:
-                        nc.scalar.activation(out=wide[n][:, t, :], in_=src, func=COPY, scale=col)
-                    else:
-                        nc.vector.tensor_scalar(out=wide[n][:, t, :], in0=src, scalar1=col, scalar2=None, op0=MULT)
+        def quantise(n, b0, b1):
+            q, g = divmod(n, G)
+            cols = slice(b0 * P, b1 * P)
+            nc.vector.quantize_mx(
+                out=p_codes[:, q, g, cols].bitcast(FP8X4),
+                scales=p_scales[:, q, g, cols],
+                in_=mixed[n][:, b0 * P * T : b1 * P * T],
+            )
 
-            def lay_pe(n):
-                if IL[n] != "P":
-                    return
-                for h in range(2):
-                    b = free.pop(0)
-                    ilb[(n, h)] = psum.tile([P, 2 * W], BF16, name=f"ilb_{n}_{h}", tag=f"bank_{b}", bufs=1)
-                    held[("il", n, h)] = b
-                    for k in range(2):
-                        i0 = (2 * h + k) * P
-                        nc.tensor.matmul(
-                            ilb[(n, h)][:, k * W : (k + 1) * W].rearrange("p (b m t) -> p m t b", b=T, t=T),
-                            lhsT=ident[:],
-                            rhs=wide[n][:, :, i0 : i0 + P].rearrange("p t (m b) -> p m t b", b=T),
-                            start=True,
-                            stop=True,
-                        )
+        def interleave_v(sweep, g, c0, c1, copy):
+            if (sweep, g) not in v_mixed:
+                v_mixed[sweep, g] = rows.tile([P, C, T], BF16, name=f"v_mixed_{sweep}_{g}", tag="v_mixed", align_bytes=64)
+            src = v_raw[:, g] if sweep == 0 else v1_rows[g][:]
+            copy(out=v_mixed[sweep, g][:, c0:c1, :], in_=src[:, :, c0:c1].rearrange("p t c -> p c t"))
 
-            def il_views(n):
-                return (
-                    inter[n][:].rearrange("p (b m e t) -> p m b e t", b=T, e=2, t=T),
-                    wide[n][:].rearrange("p t (m e b) -> p m b e t", e=2, b=T),
-                )
+        def quantise_v(sweep, g, c0, c1):
+            nc.vector.quantize_mx(
+                out=v_codes[sweep][:, g, c0:c1].bitcast(FP8X4),
+                scales=v_scales[sweep][:, g, c0:c1],
+                in_=v_mixed[sweep, g][:, c0:c1, :].rearrange("p c t -> p (c t)"),
+            )
 
-            def lay(n):
-                inter[n] = work.tile([P, W * T], BF16, name=f"inter_{n}", tag="inter", align_bytes=64)
-                dst, src = il_views(n)
-                if IL[n] == "P":
-                    for h in range(2):
-                        nc.scalar.copy(
-                            out=inter[n][:].rearrange("p (b h k x) -> p h k b x", b=T, h=2, k=2)[:, h],
-                            in_=ilb[(n, h)][:].rearrange("p (k b x) -> p k b x", k=2, b=T),
-                        )
-                        give(("il", n, h))
-                elif IL[n] == "S":
-                    nc.scalar.copy(out=dst, in_=src)
-                elif IL[n] == "V":
-                    nc.vector.tensor_copy(out=dst, in_=src)
-                else:
-                    nc.scalar.copy(out=dst[:, 40:], in_=src[:, 40:])
-                    nc.vector.tensor_copy(out=dst[:, :40], in_=src[:, :40])
-
-            def quant(n):
-                q, g = divmod(n, G)
-                nc.vector.quantize_mx(out=p_codes[:, q, g, :].bitcast(FP8X4), scales=p_planes[:, q, g, :], in_=inter[n][:])
-
-            def lay_v(sweep, g, eng, c0, c1):
-                key = (sweep, g)
-                if key not in v_in:
-                    v_in[key] = work.tile([P, C, T], BF16, name=f"v{sweep}_in_{g}", tag="v_in", align_bytes=64, bufs=2)
-                src = v_raw[:, g] if sweep == 0 else v1_rows[g][:]
-                eng(out=v_in[key][:, c0:c1, :], in_=src[:, :, c0:c1].rearrange("p t c -> p c t"))
-
-            def lay_half(k):
-                h, g = divmod(k, G)
-                n = 12 + g
-                if n not in inter:
-                    inter[n] = work.tile([P, W * T], BF16, name=f"inter_{n}", tag="inter", align_bytes=64)
-                dst, src = il_views(n)
-                dst, src = dst[:, :, 2 * h : 2 * h + 2], src[:, :, 2 * h : 2 * h + 2]
-                if HL[k] == "S":
-                    nc.scalar.copy(out=dst, in_=src)
-                else:
-                    nc.vector.tensor_copy(out=dst, in_=src)
-
-            def quant_half(k):
-                h, g = divmod(k, G)
-                cols = slice(2 * h * P, 2 * (h + 1) * P)
-                nc.vector.quantize_mx(
-                    out=p_codes[:, 3, g, cols].bitcast(FP8X4),
-                    scales=p_planes[:, 3, g, cols],
-                    in_=inter[12 + g][:, 2 * h * T * P : 2 * (h + 1) * T * P],
-                )
-
-            def quant_v(sweep, g):
-                nc.vector.quantize_mx(
-                    out=v_codes[sweep][:, g, :].bitcast(FP8X4),
-                    scales=v_planes[sweep][:, g, :],
-                    in_=v_in[(sweep, g)][:].rearrange("p c t -> p (c t)"),
-                )
-
-            def mm(acc, sweep, q, b, g, first=0, last=G - 1):
-                cols = slice(b * P, (b + 1) * P)
-                nc.tensor.matmul_mx(
-                    out=acc[:],
-                    lhsT=p_codes[:, q, g, cols].bitcast(FP8X4),
-                    lhsT_scale=p_planes[:, q, g, cols],
-                    rhs=v_codes[sweep][:, g, :].bitcast(FP8X4),
-                    rhs_scale=v_planes[sweep][:, g, :],
-                    start=(g == first),
-                    stop=(g == last),
-                )
-
-            def bank(name):
-                b = free.pop(0)
-                held[name] = b
-                return psum.tile([P, C], F32, name=name, tag=f"bank_{b}", bufs=1)
-
-            def give(name):
-                free.append(held[name])
-
-            def sweep1(q, b, g):
+        def multiply(sweep, q, b, groups):
+            cols = slice(b * P, (b + 1) * P)
+            for g in groups:
                 if g == 0:
-                    acc1[(q, b)] = bank(f"acc1_{q}_{b}")
-                mm(acc1[(q, b)], 0, q, b, g)
-
-            def update(dst, acc, q, b):
-                nc.vector.scalar_tensor_tensor(
-                    out=dst, in0=acc[:], scalar=disc[:, q * T + b : q * T + b + 1], in1=r_sb[:, q, b, :], op0=MULT, op1=ADD
+                    acc[sweep, q, b] = psum.tile([P, C], F32, name=f"acc_{sweep}_{q}_{b}", tag="bank")
+                nc.tensor.matmul_mx(
+                    out=acc[sweep, q, b][:],
+                    lhsT=p_codes[:, q, g, cols].bitcast(FP8X4),
+                    lhsT_scale=p_scales[:, q, g, cols],
+                    rhs=v_codes[sweep][:, g, :].bitcast(FP8X4),
+                    rhs_scale=v_scales[sweep][:, g, :],
+                    start=(g == 0),
+                    stop=(g == G - 1),
                 )
 
-            def evac1(q, b):
-                if b == 0:
-                    v1_rows[q] = work.tile([P, T, C], BF16, name=f"v1_rows_{q}", tag="v1_rows", align_bytes=64, bufs=2)
-                update(v1_rows[q][:, b, :], acc1[(q, b)], q, b)
-                give(f"acc1_{q}_{b}")
+        def update(dst, sweep, q, b, c0, c1):
+            nc.vector.scalar_tensor_tensor(
+                out=dst[:, c0:c1],
+                in0=acc[sweep, q, b][:, c0:c1],
+                scalar=disc[:, q, b : b + 1],
+                in1=r_sb[:, q, b, c0:c1],
+                op0=MULT,
+                op1=ADD,
+            )
 
-            def sweep2(i, gs, first=0, last=G - 1):
-                q, b = divmod(i, T)
-                for g in gs:
-                    if g == first:
-                        acc2[i] = bank(f"acc2_{i}_{g}")
-                    mm(acc2[i], 1, q, b, g, first, last)
+        def update_v1(q, b, c0, c1):
+            if q not in v1_rows:
+                v1_rows[q] = rows.tile([P, T, C], BF16, name=f"v1_rows_{q}", tag="v1_rows", align_bytes=64)
+            update(v1_rows[q][:, b, :], 0, q, b, c0, c1)
 
-            def evac1_half(q, b, half):
-                c = slice(half * HC, (half + 1) * HC)
-                if b not in done_half.setdefault(q, []):
-                    done_half[q].append(b)
-                nc.vector.scalar_tensor_tensor(
-                    out=v1_get(q)[:, b, c], in0=acc1[(q, b)][:, c], scalar=disc[:, q * T + b : q * T + b + 1], in1=r_sb[:, q, b, c], op0=MULT, op1=ADD
-                )
-                if half == 1:
-                    give(f"acc1_{q}_{b}")
+        def finish(q, b, pieces):
+            result = results.tile([P, C], F32, name=f"result_{q}_{b}", tag="result")
+            for k in range(pieces):
+                c0, c1 = k * C // pieces, (k + 1) * C // pieces
+                update(result, 1, q, b, c0, c1)
+                nc.sync.dma_start(out=out_view[q][:, b, c0:c1], in_=result[:, c0:c1])
 
-            def v1_get(q):
-                return v1_rows[q]
-
-            def quant_v_half(sweep, g, half):
-                c = slice(half * HC, (half + 1) * HC)
-                nc.vector.quantize_mx(
-                    out=v_codes[sweep][:, g, c].bitcast(FP8X4),
-                    scales=v_planes[sweep][:, g, c],
-                    in_=v_in[(sweep, g)][:, c, :].rearrange("p c t -> p (c t)"),
-                )
-
-            def spill(i):
-                q, b = divmod(i, T)
-                part[i] = keep.tile([P, C], F32, name=f"part_{i}")
-                nc.scalar.activation(out=part[i][:], in_=acc2[i][:], func=COPY, scale=disc[:, i : i + 1])
-                give(f"acc2_{i}_0")
-
-            def evac2b(i):
-                q, b = divmod(i, T)
-                o1 = outs.tile([P, C], F32, name=f"sum_{i}", tag="sum", bufs=3)
-                nc.vector.scalar_tensor_tensor(out=o1[:], in0=acc2[i][:], scalar=disc[:, i : i + 1], in1=part[i][:], op0=MULT, op1=ADD)
-                give(f"acc2_{i}_2")
-                o = outs.tile([P, C], F32, name=f"out_{i}", tag="o")
-                nc.gpsimd.tensor_tensor(out=o[:], in0=o1[:], in1=r_sb[:, q, b, :], op=ADD)
-                nc.sync.dma_start(out=o_view[q][:, b, :], in_=o[:])
-
-            def evac2(i):
-                q, b = divmod(i, T)
-                o = outs.tile([P, C], F32, name=f"out_{i}", tag="o")
-                update(o[:], acc2[i], q, b)
-                give(f"acc2_{i}_0")
-                nc.sync.dma_start(out=o_view[q][:, b, :], in_=o[:])
-
-            widen(0)
-            lay_pe(0)
-            lay_v(0, 0, COPIER[VIL[0]], 0, C)
-            widen(1)
-            lay_pe(1)
-            lay(0)
-            quant_v(0, 0)
-            lay_v(0, 1, COPIER[VIL[1]], 0, C)
-            widen(2)
-            for n in range(12):
-                q, g = divmod(n, G)
-                if n == 3:
-                    nc.vector.tensor_copy(out=disc[:], in_=disc_in[:])
-                if n + 2 < 12:
-                    lay_pe(n + 2)
-                if n + 1 < 12:
-                    lay(n + 1)
-                quant(n)
-                if q >= 1 and g == 0:
-                    for b in range(T):
-                        evac1(q - 1, b)
-                widen(n + 3)
-                if n < G:
-                    if n:
-                        quant_v(0, n)
-                    if 1 <= n + 1 < G and n:
-                        lay_v(0, n + 1, COPIER[VIL[n + 1]], 0, C)
-                if q >= 1 and g == 1:
-                    lay_v(1, q - 1, COPIER[V1IL[q - 1]], 0, C)
-                if q >= 1 and g == 2:
-                    quant_v(1, q - 1)
+        widen(0)
+        interleave_v(0, 0, 0, C, copier[V_BY[0]])
+        widen(1)
+        interleave(0, 0, T, nc.vector.tensor_copy)
+        quantise_v(0, 0, 0, C)
+        interleave_v(0, 1, 0, C, copier[V_BY[1]])
+        widen(2)
+        last = (G - 1) * G
+        for n in range(last):
+            q, g = divmod(n, G)
+            if n + 1 < last:
+                interleave(n + 1, 0, T, nc.vector.tensor_copy)
+            quantise(n, 0, T)
+            if q >= 1 and g == 0:
                 for b in range(T):
-                    sweep1(q, b, g)
-            lay_half(0)
-            widen(15)
-            for k in range(8):
-                h, g = divmod(k, G)
-                if k < 7:
-                    lay_half(k + 1)
-                quant_half(k)
-                if k == 0:
-                    for b in range(T):
-                        evac1(2, b)
-                if k == 1:
-                    lay_v(1, 2, COPIER[V1IL[2]], 0, C)
-                if k == 2:
-                    quant_v(1, 2)
-                if k == 5:
-                    evac1(3, 0)
-                    evac1(3, 1)
-                for b in (2 * h, 2 * h + 1):
-                    sweep1(3, b, g)
-                if k < 4:
-                    sweep2(k, [0, 1])
-                if k in (4, 5):
-                    sweep2(k - 4, [2])
-            for half in range(2):
-                for b in (2, 3):
-                    evac1_half(3, b, half)
-            for i in (2, 3):
-                sweep2(i, [2])
-            for i in range(4, 8):
-                sweep2(i, [0, 1, 2])
-            lay_v(1, 3, nc.scalar.copy, 0, HC)
-            lay_v(1, 3, nc.vector.tensor_copy, HC, C)
-            for half in range(2):
-                quant_v_half(1, 3, half)
-            for i in range(8):
-                sweep2(i, [3])
-                evac2(i)
-            for i in range(8, 16):
-                sweep2(i, range(G))
-                evac2(i)
+                    update_v1(q - 1, b, 0, C)
+            widen(n + 3)
+            if 1 <= n < G:
+                quantise_v(0, n, 0, C)
+                if n + 1 < G:
+                    interleave_v(0, n + 1, 0, C, copier[V_BY[n + 1]])
+            if q >= 1 and g == 1:
+                interleave_v(1, q - 1, 0, C, copier[V1_BY[q - 1]])
+            if q >= 1 and g == 2:
+                quantise_v(1, q - 1, 0, C)
+            for b in range(T):
+                multiply(0, q, b, [g])
+
+        interleave(last, 0, 2, copier[LAST_BY[0]])
+        widen(last + 3)
+        for k in range(2 * G):
+            h, g = divmod(k, G)
+            if k + 1 < 2 * G:
+                h_next, g_next = divmod(k + 1, G)
+                interleave(last + g_next, 2 * h_next, 2 * h_next + 2, copier[LAST_BY[k + 1]])
+            quantise(last + g, 2 * h, 2 * h + 2)
+            if k == 0:
+                for b in range(T):
+                    update_v1(G - 2, b, 0, C)
+            if k == 1:
+                interleave_v(1, G - 2, 0, C, copier[V1_BY[G - 2]])
+            if k == 2:
+                quantise_v(1, G - 2, 0, C)
+            if k == 5:
+                update_v1(G - 1, 0, 0, C)
+                update_v1(G - 1, 1, 0, C)
+            for b in (2 * h, 2 * h + 1):
+                multiply(0, G - 1, b, [g])
+            if h == 0:
+                multiply(1, 0, g, [0, 1])
+            if k in (4, 5):
+                multiply(1, 0, k - 4, [2])
+
+        for c0 in (0, HALF):
+            for b in (2, 3):
+                update_v1(G - 1, b, c0, c0 + HALF)
+        for b in (2, 3):
+            multiply(1, 0, b, [2])
+        for b in range(T):
+            multiply(1, 1, b, [0, 1, 2])
+        interleave_v(1, G - 1, 0, HALF, nc.scalar.copy)
+        interleave_v(1, G - 1, HALF, C, nc.vector.tensor_copy)
+        for c0 in (0, HALF):
+            quantise_v(1, G - 1, c0, c0 + HALF)
+
+        for q in range(G):
+            for b in range(T):
+                multiply(1, q, b, [G - 1] if q < 2 else range(G))
+                finish(q, b, 2 if (q, b) == (G - 1, T - 1) else 1)

from contextlib import ExitStack

import concourse.mybir as mybir

S, C = 2048, 512
P = 128
T = 4
W = P * T
G = S // W
HALF = C // 2

F32 = mybir.dt.float32
BF16 = mybir.dt.bfloat16
U32 = mybir.dt.uint32
U8 = mybir.dt.uint8
FP8 = mybir.dt.float8_e4m3fn
FP8X4 = mybir.dt.float8_e4m3fn_x4
MULT = mybir.AluOpType.mult
ADD = mybir.AluOpType.add
COPY = mybir.ActivationFunctionType.Copy

FLOPS = 2 * 2 * S * S * C

SCALAR_SLOTS = [1] + [4, 4, 3] + [4, 4, 4, 3] + [4, 4, 4, 3] + [4, 4, 4, 4]
V_BY = "VVSV"
V1_BY = "SSV"
LAST_BY = "VVVSSSVS"


def tile_two_sweep_policy_evaluation_d3_kernel(tc, P_bytes, P_scale, V, R, discount, out):
    nc = tc.nc
    copier = {"V": nc.vector.tensor_copy, "S": nc.scalar.copy}

    with ExitStack() as ctx:
        keep = ctx.enter_context(tc.tile_pool(name="keep", bufs=1))
        chunks = ctx.enter_context(tc.tile_pool(name="chunks", bufs=5))
        rows = ctx.enter_context(tc.tile_pool(name="rows", bufs=2))
        results = ctx.enter_context(tc.tile_pool(name="results", bufs=10))
        psum = ctx.enter_context(tc.psum_pool(name="psum", bufs=8))

        scale_0 = keep.tile([P, T], F32, name="scale_0")
        scale_rest = keep.tile([P, G - 1, T], F32, name="scale_rest")
        disc = keep.tile([P, G, T], BF16, name="disc")
        bytes_q = [keep.tile([P, G, T, W], U8, name=f"bytes_{q}", align_bytes=64) for q in range(2)]
        bytes_23 = keep.tile([P, G, T, 2 * W], U8, name="bytes_23", align_bytes=64)
        v_raw = keep.tile([P, G, T, C], BF16, name="v_raw", align_bytes=64)
        r_sb = keep.tile([P, G, T, C], BF16, name="r_sb", align_bytes=64)
        p_codes = keep.tile([P, G, G, W], U32, name="p_codes", align_bytes=64)
        p_scales = keep.tile([P, G, G, W], U8, name="p_scales", align_bytes=64)
        v_codes = [keep.tile([P, G, C], U32, name=f"v_codes_{s}", align_bytes=64) for s in range(2)]
        v_scales = [keep.tile([P, G, C], U8, name=f"v_scales_{s}", align_bytes=64) for s in range(2)]

        scale_view = P_scale.rearrange("(g p t) o -> p g (t o)", p=P, t=T)
        p_view = P_bytes.rearrange("(g p t) i -> g p t i", p=P, t=T)
        v_view = V.rearrange("(g p t) c -> g p t c", p=P, t=T)
        r_view = R.rearrange("(g p t) c -> g p t c", p=P, t=T)
        out_view = out.rearrange("(g p t) c -> g p t c", p=P, t=T)

        nc.scalar.dma_start(out=scale_0[:], in_=scale_view[:, 0])
        nc.sync.dma_start(out=bytes_q[0][:, 0], in_=p_view[0][:, :, 0:W])
        nc.sync.dma_start(out=scale_rest[:], in_=scale_view[:, 1:])
        nc.sync.dma_start(out=v_raw[:, 0], in_=v_view[0])
        for g in range(1, G):
            nc.sync.dma_start(out=bytes_q[0][:, g], in_=p_view[g][:, :, 0:W])
            nc.sync.dma_start(out=v_raw[:, g], in_=v_view[g])
        for g in range(G):
            nc.sync.dma_start(out=bytes_q[1][:, g], in_=p_view[g][:, :, W : 2 * W])
        nc.sync.dma_start(out=disc[:], in_=discount.rearrange("(g p t) o -> p g (t o)", p=P, t=T))
        nc.sync.dma_start(out=r_sb[:, 0], in_=r_view[0])
        for g in range(G):
            nc.sync.dma_start(out=bytes_23[:, g], in_=p_view[g][:, :, 2 * W :])
        for q in range(1, G):
            nc.sync.dma_start(out=r_sb[:, q], in_=r_view[q])

        wide = {}
        mixed = {}
        v_mixed = {}
        v1_rows = {}
        acc = {}

        def widen(n):
            q, g = divmod(n, G)
            wide[n] = chunks.tile([P, T, W], BF16, name=f"wide_{n}", tag="wide", align_bytes=64)
            for t in range(T):
                src = bytes_q[q][:, g, t, :] if q < 2 else bytes_23[:, g, t, (q - 2) * W : (q - 1) * W]
                scale = scale_0[:, t : t + 1] if g == 0 else scale_rest[:, g - 1, t : t + 1]
                if t < SCALAR_SLOTS[n]:
                    nc.scalar.activation(out=wide[n][:, t, :], in_=src.bitcast(FP8), func=COPY, scale=scale)
                else:
                    nc.vector.tensor_scalar(
                        out=wide[n][:, t, :], in0=src.bitcast(FP8), scalar1=scale, scalar2=None, op0=MULT
                    )

        def interleave(n, b0, b1, copy):
            if n not in mixed:
                mixed[n] = chunks.tile([P, W * T], BF16, name=f"mixed_{n}", tag="mixed", align_bytes=64)
            copy(
                out=mixed[n][:].rearrange("p (b m e t) -> p m b e t", b=T, e=2, t=T)[:, :, b0:b1],
                in_=wide[n][:].rearrange("p t (m e b) -> p m b e t", e=2, b=T)[:, :, b0:b1],
            )

        def quantise(n, b0, b1):
            q, g = divmod(n, G)
            cols = slice(b0 * P, b1 * P)
            nc.vector.quantize_mx(
                out=p_codes[:, q, g, cols].bitcast(FP8X4),
                scales=p_scales[:, q, g, cols],
                in_=mixed[n][:, b0 * P * T : b1 * P * T],
            )

        def interleave_v(sweep, g, c0, c1, copy):
            if (sweep, g) not in v_mixed:
                v_mixed[sweep, g] = rows.tile([P, C, T], BF16, name=f"v_mixed_{sweep}_{g}", tag="v_mixed", align_bytes=64)
            src = v_raw[:, g] if sweep == 0 else v1_rows[g][:]
            copy(out=v_mixed[sweep, g][:, c0:c1, :], in_=src[:, :, c0:c1].rearrange("p t c -> p c t"))

        def quantise_v(sweep, g, c0, c1):
            nc.vector.quantize_mx(
                out=v_codes[sweep][:, g, c0:c1].bitcast(FP8X4),
                scales=v_scales[sweep][:, g, c0:c1],
                in_=v_mixed[sweep, g][:, c0:c1, :].rearrange("p c t -> p (c t)"),
            )

        def multiply(sweep, q, b, groups):
            cols = slice(b * P, (b + 1) * P)
            for g in groups:
                if g == 0:
                    acc[sweep, q, b] = psum.tile([P, C], F32, name=f"acc_{sweep}_{q}_{b}", tag="bank")
                nc.tensor.matmul_mx(
                    out=acc[sweep, q, b][:],
                    lhsT=p_codes[:, q, g, cols].bitcast(FP8X4),
                    lhsT_scale=p_scales[:, q, g, cols],
                    rhs=v_codes[sweep][:, g, :].bitcast(FP8X4),
                    rhs_scale=v_scales[sweep][:, g, :],
                    start=(g == 0),
                    stop=(g == G - 1),
                )

        def update(dst, sweep, q, b, c0, c1):
            nc.vector.scalar_tensor_tensor(
                out=dst[:, c0:c1],
                in0=acc[sweep, q, b][:, c0:c1],
                scalar=disc[:, q, b : b + 1],
                in1=r_sb[:, q, b, c0:c1],
                op0=MULT,
                op1=ADD,
            )

        def update_v1(q, b, c0, c1):
            if q not in v1_rows:
                v1_rows[q] = rows.tile([P, T, C], BF16, name=f"v1_rows_{q}", tag="v1_rows", align_bytes=64)
            update(v1_rows[q][:, b, :], 0, q, b, c0, c1)

        def finish(q, b, pieces):
            result = results.tile([P, C], F32, name=f"result_{q}_{b}", tag="result")
            for k in range(pieces):
                c0, c1 = k * C // pieces, (k + 1) * C // pieces
                update(result, 1, q, b, c0, c1)
                nc.sync.dma_start(out=out_view[q][:, b, c0:c1], in_=result[:, c0:c1])

        widen(0)
        interleave_v(0, 0, 0, C, copier[V_BY[0]])
        widen(1)
        interleave(0, 0, T, nc.vector.tensor_copy)
        quantise_v(0, 0, 0, C)
        interleave_v(0, 1, 0, C, copier[V_BY[1]])
        widen(2)
        last = (G - 1) * G
        for n in range(last):
            q, g = divmod(n, G)
            if n + 1 < last:
                interleave(n + 1, 0, T, nc.vector.tensor_copy)
            quantise(n, 0, T)
            if q >= 1 and g == 0:
                for b in range(T):
                    update_v1(q - 1, b, 0, C)
            widen(n + 3)
            if 1 <= n < G:
                quantise_v(0, n, 0, C)
                if n + 1 < G:
                    interleave_v(0, n + 1, 0, C, copier[V_BY[n + 1]])
            if q >= 1 and g == 1:
                interleave_v(1, q - 1, 0, C, copier[V1_BY[q - 1]])
            if q >= 1 and g == 2:
                quantise_v(1, q - 1, 0, C)
            for b in range(T):
                multiply(0, q, b, [g])

        interleave(last, 0, 2, copier[LAST_BY[0]])
        widen(last + 3)
        for k in range(2 * G):
            h, g = divmod(k, G)
            if k + 1 < 2 * G:
                h_next, g_next = divmod(k + 1, G)
                interleave(last + g_next, 2 * h_next, 2 * h_next + 2, copier[LAST_BY[k + 1]])
            quantise(last + g, 2 * h, 2 * h + 2)
            if k == 0:
                for b in range(T):
                    update_v1(G - 2, b, 0, C)
            if k == 1:
                interleave_v(1, G - 2, 0, C, copier[V1_BY[G - 2]])
            if k == 2:
                quantise_v(1, G - 2, 0, C)
            if k == 5:
                update_v1(G - 1, 0, 0, C)
                update_v1(G - 1, 1, 0, C)
            for b in (2 * h, 2 * h + 1):
                multiply(0, G - 1, b, [g])
            if h == 0:
                multiply(1, 0, g, [0, 1])
            if k in (4, 5):
                multiply(1, 0, k - 4, [2])

        for c0 in (0, HALF):
            for b in (2, 3):
                update_v1(G - 1, b, c0, c0 + HALF)
        for b in (2, 3):
            multiply(1, 0, b, [2])
        for b in range(T):
            multiply(1, 1, b, [0, 1, 2])
        interleave_v(1, G - 1, 0, HALF, nc.scalar.copy)
        interleave_v(1, G - 1, HALF, C, nc.vector.tensor_copy)
        for c0 in (0, HALF):
            quantise_v(1, G - 1, c0, c0 + HALF)

        for q in range(G):
            for b in range(T):
                multiply(1, q, b, [G - 1] if q < 2 else range(G))
                finish(q, b, 2 if (q, b) == (G - 1, T - 1) else 1)
